import numpy as np
import ml_dtypes


def mxq(x, axis, fmt="e4m3"):
    dtype, down = {"e4m3": (ml_dtypes.float8_e4m3fn, 7), "e5m2": (ml_dtypes.float8_e5m2, 14)}[fmt]
    v = np.moveaxis(np.asarray(x, np.float32).astype(ml_dtypes.bfloat16).astype(np.float64), axis, -1)
    blocks = v.reshape(v.shape[:-1] + (-1, 32))
    amax = np.abs(blocks).max(-1, keepdims=True)
    byte = np.maximum(np.where(amax > 0, np.frexp(amax)[1] - 1 + 127, 0) - down, 1)
    scale = np.exp2(byte - 127.0)
    codes = (blocks / scale).astype(np.float32).astype(dtype).astype(np.float64)
    return np.moveaxis((codes * scale).reshape(v.shape), -1, axis)


WIDE = False


def mx_kscale(k):
    if not WIDE:
        return np.ones(k)
    levels = np.array([10, -10, 5, -5, 0])
    if k % 512:
        return np.exp2(np.random.permutation(np.resize(levels, k // 32))).repeat(32)
    a = np.empty((k // 512, 16))
    for p in range(k // 512):
        a[p, :8] = np.random.permutation(np.resize(levels, 8))
        for g in range(8):
            far = levels[np.abs(levels - a[p, g]) >= 10]
            a[p, g + 8] = far[np.random.randint(len(far))]
    return np.exp2(a.ravel()).repeat(32)


def f64(x):
    return np.asarray(x).astype(np.float64)


def striped(idx):
    return np.tile(idx.reshape(-1, 16).T, (8, 1)).astype(np.uint16)


def unstriped(offs):
    return offs[:16].T.reshape(-1).astype(np.int64)


def striped8(idx):
    return np.concatenate([x.reshape(-1, 16).T for x in idx]).astype(np.uint16)


def runs(offs, k):
    lists = np.stack([offs[16 * r : 16 * r + 16].T.reshape(-1) for r in range(8)]).astype(np.int64)
    return lists[np.arange(k) % 512 // 64]


def pack_weight(w):
    k, n = w.shape
    w = f64(np.asarray(w, np.float32).astype(ml_dtypes.bfloat16)).reshape(k // 32, 32, n)
    amax = np.abs(w).max(1)
    byte = np.clip(np.where(amax > 0, np.frexp(amax)[1] - 1 + 127 - 7, 1), 1, 254)
    scaled = (w * np.exp2(127.0 - byte)[:, None, :]).reshape(k, n).astype(np.float32)
    words = np.ascontiguousarray(scaled.reshape(k // 512, 128, 4, n).transpose(0, 1, 3, 2)).astype(ml_dtypes.float8_e4m3fn).view(np.uint8)
    return words, np.ascontiguousarray(byte.astype(np.uint8).reshape(k // 512, 16, n))


def unpack_weight(words, scales):
    g, p, n, _ = words.shape
    vals = np.ascontiguousarray(words).view(ml_dtypes.float8_e4m3fn).astype(np.float64) * np.repeat(np.exp2(scales.astype(np.float64) - 127.0), 8, axis=1)[..., None]
    return vals.transpose(0, 1, 3, 2).reshape(g * 512, n)


E2M1 = np.array([0.0, 0.5, 1.0, 1.5, 2.0, 3.0, 4.0, 6.0, -0.0, -0.5, -1.0, -1.5, -2.0, -3.0, -4.0, -6.0])


def pack_fp4(w):
    k, n = w.shape
    w = f64(np.asarray(w, np.float32).astype(ml_dtypes.bfloat16)).reshape(k // 32, 32, n)
    amax = np.abs(w).max(1)
    mant, ex = np.frexp(amax / 6.0)
    byte = np.clip(np.where(amax > 0, np.where(mant > 0.5, ex, ex - 1) + 127, 1), 1, 254)
    scaled = (w * np.exp2(127.0 - byte)[:, None, :]).reshape(k, n).astype(np.float32)
    c = np.ascontiguousarray(scaled.reshape(k // 512, 128, 4, n).transpose(0, 1, 3, 2)).astype(ml_dtypes.float4_e2m1fn).view(np.uint8) & 0xF
    words = (c[..., 0::2] | (c[..., 1::2] << 4)).reshape(k // 512, 128, 2 * n)
    return np.ascontiguousarray(words), np.ascontiguousarray(byte.astype(np.uint8).reshape(k // 512, 16, n))


def unpack_fp4(words, scales):
    g, _, n = scales.shape
    words = np.ascontiguousarray(words).reshape(g, 128, n, 2)
    nib = np.empty((g, 128, n, 4), np.uint8)
    nib[..., 0::2] = words & 0xF
    nib[..., 1::2] = words >> 4
    vals = E2M1[nib] * np.repeat(np.exp2(scales.astype(np.float64) - 127.0), 8, axis=1)[..., None]
    return vals.transpose(0, 1, 3, 2).reshape(g * 512, n)


def sigmoid(v):
    return 1.0 / (1.0 + np.exp(-np.maximum(v, -700.0)))


K, T, S, N, G, H = 512, 2048, 256, 512, 2048, 512


def setup_inputs():
    n = np.random.standard_normal
    s = mx_kscale(K)[:, None]
    u = mx_kscale(K)
    packed_xT = pack_weight(n((K, T)) * s)
    packed_dT = pack_weight(n((K, G)) / s)
    packed_w1 = pack_fp4(n((H, N)) / np.sqrt(H) / u[:, None])
    return {
        "x_words": packed_xT[0],
        "x_scales": packed_xT[1],
        "d_words": packed_dT[0],
        "d_scales": packed_dT[1],
        "gn": (np.random.uniform(0.5, 1.5, (H, 1)) * u[:, None]).astype(np.float32),
        "w1_words": packed_w1[0],
        "w1_scales": packed_w1[1],
        "sl": np.random.uniform(1.0, 2.0, (N, 1)).astype(np.float32),
        "th": (0.5 * n((N, 1))).astype(np.float32),
        "offs": striped8(np.random.randint(0, T, (8, S))),
        "ci": striped(np.random.permutation(G)[:H]),
        "n1": striped(np.random.permutation(S)),
        "n2": striped(np.random.permutation(S)),
        "n3": striped(np.random.permutation(S)),
        "n4": striped(np.random.permutation(S)),
    }


def reference(x_words, x_scales, d_words, d_scales, gn, w1_words, w1_scales, sl, th, offs, ci, n1, n2, n3, n4):
    d_ci = unpack_weight(d_words, d_scales)[:, unstriped(ci)]
    xq = unpack_weight(x_words, x_scales)[np.arange(K)[:, None], runs(offs, K)]
    s = 0.0625 * (d_ci.T @ xq)
    st = np.maximum(s, s[:, unstriped(n1)])
    ds = np.zeros((H, S))
    ds[:, unstriped(n2)] = st
    z = f64(gn) * (ds - s)
    h = unpack_fp4(w1_words, w1_scales).T @ mxq(z, 0, "e4m3")
    ds2 = np.zeros((N, S))
    ds2[:, unstriped(n3)] = h
    sg = sigmoid(f64(sl) * (ds2[:, unstriped(n4)] - f64(th)))
    return h * sg

@@ -1,0 +1,175 @@
+from contextlib import ExitStack
+
+import concourse.mybir as mybir
+
+K, T, S, N, G, H = 512, 2048, 256, 512, 2048, 512
+FLOPS = 2 * K * H * S + 2 * H * N * S
+
+F32 = mybir.dt.float32
+BF16 = mybir.dt.bfloat16
+I32 = mybir.dt.int32
+U32 = mybir.dt.uint32
+U16 = mybir.dt.uint16
+U8 = mybir.dt.uint8
+FP8X4 = mybir.dt.float8_e4m3fn_x4
+FP4X4 = mybir.dt.float4_e2m1fn_x4
+ALU = mybir.AluOpType
+ACT = mybir.ActivationFunctionType
+
+P = 128
+PACK = 4
+HALF = S // 2
+WIDE = 2 * S
+
+
+def tile_picked_hwlsendhoperl_none_p_kernel(
+    tc, x_words, x_scales, d_words, d_scales, gn, w1_words, w1_scales, sl, th, offs, ci, n1, n2, n3, n4, out
+):
+    nc = tc.nc
+    with ExitStack() as ctx:
+        keep = ctx.enter_context(tc.tile_pool(name="keep", bufs=1))
+        reuse = ctx.enter_context(tc.tile_pool(name="reuse", bufs=1))
+        psum = ctx.enter_context(tc.psum_pool(name="psum", bufs=8))
+
+        def load_list(name, src):
+            tile = keep.tile([P, src.shape[1]], U16, name=name)
+            nc.sync.dma_start(tile[:], src)
+            return tile
+
+        x_bytes = keep.tile([P, T], U8, align_bytes=64)
+        d_bytes = keep.tile([P, G], U8, align_bytes=64)
+        nc.vector.memset(x_bytes[:].bitcast(I32), 0)
+        nc.vector.memset(d_bytes[:].bitcast(I32), 0)
+        offs_sb = load_list("offs_sb", offs)
+        ci_sb = load_list("ci_sb", ci)
+        n1_sb = load_list("n1_sb", n1)
+        n2_sb = load_list("n2_sb", n2)
+        nc.sync.dma_start(x_bytes[0:P:8, :].bitcast(I32), x_scales[0].bitcast(I32))
+        nc.sync.dma_start(d_bytes[0:P:8, :].bitcast(I32), d_scales[0].bitcast(I32))
+
+        d_table = keep.tile([P, G], U32, align_bytes=64)
+        x_table = reuse.tile([P, T], U32, align_bytes=64, offset=0)
+        nc.sync.dma_start(d_table[:].bitcast(I32), d_words[0].rearrange("p n r -> p (n r)").bitcast(I32))
+        nc.sync.dma_start(x_table[:].bitcast(I32), x_words[0].rearrange("p n r -> p (n r)").bitcast(I32))
+
+        picked_bytes = keep.tile([P, S + H], U8, align_bytes=64)
+        planes = keep.tile([P, S + H], U8, align_bytes=64)
+        nc.vector.memset(planes[:].bitcast(I32), 0)
+        nc.vector.tensor_copy(picked_bytes[:, 0:S], x_bytes[:].indirect(offs_sb[:]))
+        nc.vector.tensor_copy(
+            picked_bytes[:, S : S + H].rearrange("p (t m) -> p m t", t=PACK), d_bytes[:].indirect(ci_sb[:])
+        )
+        for r in range(PACK):
+            nc.scalar.dma_start(planes[r:P:32, :].bitcast(I32), picked_bytes[8 * r : P : 32, :].bitcast(I32))
+
+        d_codes = keep.tile([P, H], U32, align_bytes=64)
+        x_codes = keep.tile([P, S], U32, align_bytes=64)
+        nc.vector.tensor_copy(d_codes[:].rearrange("p (t m) -> p m t", t=PACK), d_table[:].indirect(ci_sb[:]))
+        nc.vector.tensor_copy(x_codes[:], x_table[:].indirect(offs_sb[:]))
+
+        gn_sb = reuse.tile([P, PACK], F32, align_bytes=64, offset=3 * N)
+        nc.sync.dma_start(gn_sb[:], gn.rearrange("(p t) o -> p (t o)", t=PACK))
+        w_codes = reuse.tile([P, 2 * N], U8, align_bytes=64, offset=0)
+        w_plane = reuse.tile([P, N], U8, align_bytes=64, offset=2 * N)
+        nc.vector.memset(w_plane[:].bitcast(I32), 0)
+        nc.sync.dma_start(w_codes[:].bitcast(I32), w1_words[0].bitcast(I32))
+        for r in range(PACK):
+            nc.sync.dma_start(w_plane[r:P:32, :].bitcast(I32), w1_scales[0, r:16:4, :].bitcast(I32))
+        n3_sb = load_list("n3_sb", n3)
+        n4_sb = load_list("n4_sb", n4)
+        sl_sb = reuse.tile([P, PACK], F32, align_bytes=64, offset=3 * N + 64)
+        th_sb = reuse.tile([P, PACK], F32, align_bytes=64, offset=3 * N + 128)
+        with nc.allow_non_contiguous_dma(reason="one value a partition and tile"):
+            nc.sync.dma_start(sl_sb[:], sl.rearrange("(t p) o -> p (t o)", p=P))
+            nc.sync.dma_start(th_sb[:], th.rearrange("(t p) o -> p (t o)", p=P))
+
+        s, fetched, st, ds, gs = [], [], [], [], []
+        for t in range(PACK):
+            acc = psum.tile([P, S], F32, name="acc")
+            nc.tensor.matmul_mx(
+                out=acc[:],
+                lhsT=d_codes[:, P * t : P * (t + 1)].bitcast(FP8X4),
+                lhsT_scale=planes[:, S + P * t : S + P * (t + 1)],
+                rhs=x_codes[:].bitcast(FP8X4),
+                rhs_scale=planes[:, 0:S],
+                start=True,
+                stop=True,
+            )
+            s.append(keep.tile([P, WIDE], F32, name=f"s{t}"))
+            nc.vector.tensor_scalar(s[t][:, 0:S], acc[:], 0.0625, None, ALU.mult)
+        for t in range(PACK):
+            fetched.append(keep.tile([P, S], F32, name=f"fetched{t}"))
+            nc.scalar.activation(fetched[t][:], s[t][:].indirect(n1_sb[:]), ACT.Copy)
+            st.append(keep.tile([P, S], F32, name=f"st{t}"))
+            nc.vector.tensor_tensor(st[t][:], s[t][:, 0:S], fetched[t][:], ALU.max)
+        for t in range(PACK):
+            gs.append(keep.tile([P, S], F32, name=f"gs{t}"))
+            nc.vector.tensor_scalar(gs[t][:], s[t][:, 0:S], gn_sb[:, t : t + 1], None, ALU.mult)
+        bias = keep.tile([P, PACK], F32)
+        nc.vector.scalar_tensor_tensor(bias[:], sl_sb[:], -1.0, th_sb[:], ALU.mult, ALU.mult)
+
+        z = keep.tile([P, S * PACK], BF16, align_bytes=64)
+        z_by_slot = z[:].rearrange("p (j t) -> p j t", t=PACK)
+        z_codes = keep.tile([P, S], U32, align_bytes=64)
+        z_plane = keep.tile([P, S], U8, align_bytes=64)
+
+        def make_z(t, j0, j1):
+            nc.vector.scalar_tensor_tensor(
+                z_by_slot[:, j0:j1, t], ds[t][:, j0:j1], gn_sb[:, t : t + 1], gs[t][:, j0:j1], ALU.mult, ALU.subtract
+            )
+
+        for t in range(PACK):
+            ds.append(keep.tile([P, WIDE], F32, name=f"ds{t}"))
+            nc.scalar.activation(ds[t][:].indirect(n2_sb[:]), st[t][:], ACT.Copy)
+            if t < PACK - 1:
+                make_z(t, 0, S)
+        for j0 in (0, HALF):
+            make_z(PACK - 1, j0, j0 + HALF)
+            nc.vector.quantize_mx(
+                out=z_codes[:, j0 : j0 + HALF].bitcast(FP8X4),
+                scales=z_plane[:, j0 : j0 + HALF],
+                in_=z[:, PACK * j0 : PACK * (j0 + HALF)],
+            )
+
+        h = [keep.tile([P, S], F32, name=f"h{m}") for m in range(PACK)]
+        ds2 = [keep.tile([P, WIDE], F32, name=f"ds2_{m}") for m in range(PACK)]
+        sg = [keep.tile([P, S], F32, name=f"sg{m}") for m in range(PACK)]
+        res = [keep.tile([P, S], F32, name=f"res{m}") for m in range(PACK)]
+
+        def product(m, j0, j1):
+            acc = psum.tile([P, j1 - j0], F32, name="acc")
+            nc.tensor.matmul_mx(
+                out=acc[:],
+                lhsT=w_codes[:, 2 * P * m : 2 * P * (m + 1)].bitcast(FP4X4),
+                lhsT_scale=w_plane[:, P * m : P * (m + 1)],
+                rhs=z_codes[:, j0:j1].bitcast(FP8X4),
+                rhs_scale=z_plane[:, j0:j1],
+                start=True,
+                stop=True,
+            )
+            return acc
+
+        def send(m, j0, j1):
+            nc.scalar.activation(ds2[m][:].indirect(n3_sb[:, j0 // 16 : j1 // 16]), h[m][:, j0:j1], ACT.Copy)
+
+        def finish(m, j0, j1):
+            nc.scalar.activation(
+                sg[m][:, j0:j1],
+                ds2[m][:].indirect(n4_sb[:, j0 // 16 : j1 // 16]),
+                ACT.Sigmoid,
+                bias=bias[:, m : m + 1],
+                scale=sl_sb[:, m : m + 1],
+            )
+            nc.vector.tensor_tensor(res[m][:, j0:j1], h[m][:, j0:j1], sg[m][:, j0:j1], ALU.mult)
+            nc.sync.dma_start(out[P * m : P * (m + 1), j0:j1], res[m][:, j0:j1])
+
+        nc.scalar.copy(h[0][:, 0:HALF], product(0, 0, HALF)[:])
+        send(0, 0, HALF)
+        nc.vector.tensor_copy(h[0][:, HALF:S], product(0, HALF, S)[:])
+        send(0, HALF, S)
+        for m in range(1, PACK):
+            nc.vector.tensor_copy(h[m][:], product(m, 0, S)[:])
+            send(m, 0, S)
+            finish(m - 1, 0, S)
+        finish(PACK - 1, 0, HALF)
+        finish(PACK - 1, HALF, S)

@@ -40,6 +40,10 @@ def tile_picked_hwlsendhoperl_none_p_kernel(
         d_bytes = keep.tile([P, G], U8, align_bytes=64)
         nc.vector.memset(x_bytes[:].bitcast(I32), 0)
         nc.vector.memset(d_bytes[:].bitcast(I32), 0)
+        warm_in = keep.tile([P, 1], F32)
+        warm_out = keep.tile([P, 1], F32)
+        nc.gpsimd.memset(warm_in[:], 0.0)
+        nc.scalar.activation(warm_out[:], warm_in[:], ACT.Sigmoid)
         offs_sb = load_list("offs_sb", offs)
         ci_sb = load_list("ci_sb", ci)
         n1_sb = load_list("n1_sb", n1)

@@ -20,6 +20,7 @@ P = 128
 PACK = 4
 HALF = S // 2
 WIDE = 2 * S
+LEAD = 512
 
 
 def tile_picked_hwlsendhoperl_none_p_kernel(
@@ -44,16 +45,17 @@ def tile_picked_hwlsendhoperl_none_p_kernel(
         warm_out = keep.tile([P, 1], F32)
         nc.gpsimd.memset(warm_in[:], 0.0)
         nc.scalar.activation(warm_out[:], warm_in[:], ACT.Sigmoid)
+        d_table = keep.tile([P, G], U32, align_bytes=64)
+        d_rows = d_words[0].rearrange("p n r -> p (n r)").bitcast(I32)
+        nc.sync.dma_start(d_table[:, 0:LEAD].bitcast(I32), d_rows[:, 0:LEAD])
         offs_sb = load_list("offs_sb", offs)
         ci_sb = load_list("ci_sb", ci)
         n1_sb = load_list("n1_sb", n1)
-        n2_sb = load_list("n2_sb", n2)
         nc.sync.dma_start(x_bytes[0:P:8, :].bitcast(I32), x_scales[0].bitcast(I32))
         nc.sync.dma_start(d_bytes[0:P:8, :].bitcast(I32), d_scales[0].bitcast(I32))
 
-        d_table = keep.tile([P, G], U32, align_bytes=64)
         x_table = reuse.tile([P, T], U32, align_bytes=64, offset=0)
-        nc.sync.dma_start(d_table[:].bitcast(I32), d_words[0].rearrange("p n r -> p (n r)").bitcast(I32))
+        nc.sync.dma_start(d_table[:, LEAD:G].bitcast(I32), d_rows[:, LEAD:G])
         nc.sync.dma_start(x_table[:].bitcast(I32), x_words[0].rearrange("p n r -> p (n r)").bitcast(I32))
 
         picked_bytes = keep.tile([P, S + H], U8, align_bytes=64)
@@ -64,13 +66,14 @@ def tile_picked_hwlsendhoperl_none_p_kernel(
             picked_bytes[:, S : S + H].rearrange("p (t m) -> p m t", t=PACK), d_bytes[:].indirect(ci_sb[:])
         )
         for r in range(PACK):
-            nc.scalar.dma_start(planes[r:P:32, :].bitcast(I32), picked_bytes[8 * r : P : 32, :].bitcast(I32))
+            (nc.scalar, nc.sync)[r % 2].dma_start(planes[r:P:32, :].bitcast(I32), picked_bytes[8 * r : P : 32, :].bitcast(I32))
 
         d_codes = keep.tile([P, H], U32, align_bytes=64)
         x_codes = keep.tile([P, S], U32, align_bytes=64)
         nc.vector.tensor_copy(d_codes[:].rearrange("p (t m) -> p m t", t=PACK), d_table[:].indirect(ci_sb[:]))
         nc.vector.tensor_copy(x_codes[:], x_table[:].indirect(offs_sb[:]))
 
+        n2_sb = load_list("n2_sb", n2)
         gn_sb = reuse.tile([P, PACK], F32, align_bytes=64, offset=3 * N)
         nc.sync.dma_start(gn_sb[:], gn.rearrange("(p t) o -> p (t o)", t=PACK))
         w_codes = reuse.tile([P, 2 * N], U8, align_bytes=64, offset=0)
@@ -88,19 +91,26 @@ def tile_picked_hwlsendhoperl_none_p_kernel(
             nc.sync.dma_start(th_sb[:], th.rearrange("(t p) o -> p (t o)", p=P))
 
         s, fetched, st, ds, gs = [], [], [], [], []
-        for t in range(PACK):
-            acc = psum.tile([P, S], F32, name="acc")
+
+        def scores(t, j0, j1):
+            acc = psum.tile([P, j1 - j0], F32, name="acc")
             nc.tensor.matmul_mx(
                 out=acc[:],
                 lhsT=d_codes[:, P * t : P * (t + 1)].bitcast(FP8X4),
                 lhsT_scale=planes[:, S + P * t : S + P * (t + 1)],
-                rhs=x_codes[:].bitcast(FP8X4),
-                rhs_scale=planes[:, 0:S],
+                rhs=x_codes[:, j0:j1].bitcast(FP8X4),
+                rhs_scale=planes[:, j0:j1],
                 start=True,
                 stop=True,
             )
+            return acc
+
+        for t in range(PACK):
             s.append(keep.tile([P, WIDE], F32, name=f"s{t}"))
-            nc.vector.tensor_scalar(s[t][:, 0:S], acc[:], 0.0625, None, ALU.mult)
+        nc.scalar.activation(s[0][:, 0:HALF], scores(0, 0, HALF)[:], ACT.Copy, scale=0.0625)
+        nc.vector.tensor_scalar(s[0][:, HALF:S], scores(0, HALF, S)[:], 0.0625, None, ALU.mult)
+        for t in range(1, PACK):
+            nc.vector.tensor_scalar(s[t][:, 0:S], scores(t, 0, S)[:], 0.0625, None, ALU.mult)
         for t in range(PACK):
             fetched.append(keep.tile([P, S], F32, name=f"fetched{t}"))
             nc.scalar.activation(fetched[t][:], s[t][:].indirect(n1_sb[:]), ACT.Copy)
@@ -167,11 +177,15 @@ def tile_picked_hwlsendhoperl_none_p_kernel(
             nc.vector.tensor_tensor(res[m][:, j0:j1], h[m][:, j0:j1], sg[m][:, j0:j1], ALU.mult)
             nc.sync.dma_start(out[P * m : P * (m + 1), j0:j1], res[m][:, j0:j1])
 
-        nc.scalar.copy(h[0][:, 0:HALF], product(0, 0, HALF)[:])
-        send(0, 0, HALF)
-        nc.vector.tensor_copy(h[0][:, HALF:S], product(0, HALF, S)[:])
-        send(0, HALF, S)
-        for m in range(1, PACK):
+        for m in (0, 1):
+            nc.scalar.copy(h[m][:, 0:HALF], product(m, 0, HALF)[:])
+        for m in (0, 1):
+            send(m, 0, HALF)
+        for m in (0, 1):
+            nc.vector.tensor_copy(h[m][:, HALF:S], product(m, HALF, S)[:])
+            send(m, HALF, S)
+        finish(0, 0, S)
+        for m in range(2, PACK):
             nc.vector.tensor_copy(h[m][:], product(m, 0, S)[:])
             send(m, 0, S)
             finish(m - 1, 0, S)

from contextlib import ExitStack

import concourse.mybir as mybir

K, T, S, N, G, H = 512, 2048, 256, 512, 2048, 512
FLOPS = 2 * K * H * S + 2 * H * N * S

F32 = mybir.dt.float32
BF16 = mybir.dt.bfloat16
I32 = mybir.dt.int32
U32 = mybir.dt.uint32
U16 = mybir.dt.uint16
U8 = mybir.dt.uint8
FP8X4 = mybir.dt.float8_e4m3fn_x4
FP4X4 = mybir.dt.float4_e2m1fn_x4
ALU = mybir.AluOpType
ACT = mybir.ActivationFunctionType

P = 128
PACK = 4
HALF = S // 2
WIDE = 2 * S
LEAD = 512


def tile_picked_hwlsendhoperl_none_p_kernel(
    tc, x_words, x_scales, d_words, d_scales, gn, w1_words, w1_scales, sl, th, offs, ci, n1, n2, n3, n4, out
):
    nc = tc.nc
    with ExitStack() as ctx:
        keep = ctx.enter_context(tc.tile_pool(name="keep", bufs=1))
        reuse = ctx.enter_context(tc.tile_pool(name="reuse", bufs=1))
        psum = ctx.enter_context(tc.psum_pool(name="psum", bufs=8))

        def load_list(name, src):
            tile = keep.tile([P, src.shape[1]], U16, name=name)
            nc.sync.dma_start(tile[:], src)
            return tile

        x_bytes = keep.tile([P, T], U8, align_bytes=64)
        d_bytes = keep.tile([P, G], U8, align_bytes=64)
        nc.vector.memset(x_bytes[:].bitcast(I32), 0)
        nc.vector.memset(d_bytes[:].bitcast(I32), 0)
        warm_in = keep.tile([P, 1], F32)
        warm_out = keep.tile([P, 1], F32)
        nc.gpsimd.memset(warm_in[:], 0.0)
        nc.scalar.activation(warm_out[:], warm_in[:], ACT.Sigmoid)
        d_table = keep.tile([P, G], U32, align_bytes=64)
        d_rows = d_words[0].rearrange("p n r -> p (n r)").bitcast(I32)
        nc.sync.dma_start(d_table[:, 0:LEAD].bitcast(I32), d_rows[:, 0:LEAD])
        offs_sb = load_list("offs_sb", offs)
        ci_sb = load_list("ci_sb", ci)
        n1_sb = load_list("n1_sb", n1)
        nc.sync.dma_start(x_bytes[0:P:8, :].bitcast(I32), x_scales[0].bitcast(I32))
        nc.sync.dma_start(d_bytes[0:P:8, :].bitcast(I32), d_scales[0].bitcast(I32))

        x_table = reuse.tile([P, T], U32, align_bytes=64, offset=0)
        nc.sync.dma_start(d_table[:, LEAD:G].bitcast(I32), d_rows[:, LEAD:G])
        nc.sync.dma_start(x_table[:].bitcast(I32), x_words[0].rearrange("p n r -> p (n r)").bitcast(I32))

        picked_bytes = keep.tile([P, S + H], U8, align_bytes=64)
        planes = keep.tile([P, S + H], U8, align_bytes=64)
        nc.vector.memset(planes[:].bitcast(I32), 0)
        nc.vector.tensor_copy(picked_bytes[:, 0:S], x_bytes[:].indirect(offs_sb[:]))
        nc.vector.tensor_copy(
            picked_bytes[:, S : S + H].rearrange("p (t m) -> p m t", t=PACK), d_bytes[:].indirect(ci_sb[:])
        )
        for r in range(PACK):
            (nc.scalar, nc.sync)[r % 2].dma_start(planes[r:P:32, :].bitcast(I32), picked_bytes[8 * r : P : 32, :].bitcast(I32))

        d_codes = keep.tile([P, H], U32, align_bytes=64)
        x_codes = keep.tile([P, S], U32, align_bytes=64)
        nc.vector.tensor_copy(d_codes[:].rearrange("p (t m) -> p m t", t=PACK), d_table[:].indirect(ci_sb[:]))
        nc.vector.tensor_copy(x_codes[:], x_table[:].indirect(offs_sb[:]))

        n2_sb = load_list("n2_sb", n2)
        gn_sb = reuse.tile([P, PACK], F32, align_bytes=64, offset=3 * N)
        nc.sync.dma_start(gn_sb[:], gn.rearrange("(p t) o -> p (t o)", t=PACK))
        w_codes = reuse.tile([P, 2 * N], U8, align_bytes=64, offset=0)
        w_plane = reuse.tile([P, N], U8, align_bytes=64, offset=2 * N)
        nc.vector.memset(w_plane[:].bitcast(I32), 0)
        nc.sync.dma_start(w_codes[:].bitcast(I32), w1_words[0].bitcast(I32))
        for r in range(PACK):
            nc.sync.dma_start(w_plane[r:P:32, :].bitcast(I32), w1_scales[0, r:16:4, :].bitcast(I32))
        n3_sb = load_list("n3_sb", n3)
        n4_sb = load_list("n4_sb", n4)
        sl_sb = reuse.tile([P, PACK], F32, align_bytes=64, offset=3 * N + 64)
        th_sb = reuse.tile([P, PACK], F32, align_bytes=64, offset=3 * N + 128)
        with nc.allow_non_contiguous_dma(reason="one value a partition and tile"):
            nc.sync.dma_start(sl_sb[:], sl.rearrange("(t p) o -> p (t o)", p=P))
            nc.sync.dma_start(th_sb[:], th.rearrange("(t p) o -> p (t o)", p=P))

        s, fetched, st, ds, gs = [], [], [], [], []

        def scores(t, j0, j1):
            acc = psum.tile([P, j1 - j0], F32, name="acc")
            nc.tensor.matmul_mx(
                out=acc[:],
                lhsT=d_codes[:, P * t : P * (t + 1)].bitcast(FP8X4),
                lhsT_scale=planes[:, S + P * t : S + P * (t + 1)],
                rhs=x_codes[:, j0:j1].bitcast(FP8X4),
                rhs_scale=planes[:, j0:j1],
                start=True,
                stop=True,
            )
            return acc

        for t in range(PACK):
            s.append(keep.tile([P, WIDE], F32, name=f"s{t}"))
        nc.scalar.activation(s[0][:, 0:HALF], scores(0, 0, HALF)[:], ACT.Copy, scale=0.0625)
        nc.vector.tensor_scalar(s[0][:, HALF:S], scores(0, HALF, S)[:], 0.0625, None, ALU.mult)
        for t in range(1, PACK):
            nc.vector.tensor_scalar(s[t][:, 0:S], scores(t, 0, S)[:], 0.0625, None, ALU.mult)
        for t in range(PACK):
            fetched.append(keep.tile([P, S], F32, name=f"fetched{t}"))
            nc.scalar.activation(fetched[t][:], s[t][:].indirect(n1_sb[:]), ACT.Copy)
            st.append(keep.tile([P, S], F32, name=f"st{t}"))
            nc.vector.tensor_tensor(st[t][:], s[t][:, 0:S], fetched[t][:], ALU.max)
        for t in range(PACK):
            gs.append(keep.tile([P, S], F32, name=f"gs{t}"))
            nc.vector.tensor_scalar(gs[t][:], s[t][:, 0:S], gn_sb[:, t : t + 1], None, ALU.mult)
        bias = keep.tile([P, PACK], F32)
        nc.vector.scalar_tensor_tensor(bias[:], sl_sb[:], -1.0, th_sb[:], ALU.mult, ALU.mult)

        z = keep.tile([P, S * PACK], BF16, align_bytes=64)
        z_by_slot = z[:].rearrange("p (j t) -> p j t", t=PACK)
        z_codes = keep.tile([P, S], U32, align_bytes=64)
        z_plane = keep.tile([P, S], U8, align_bytes=64)

        def make_z(t, j0, j1):
            nc.vector.scalar_tensor_tensor(
                z_by_slot[:, j0:j1, t], ds[t][:, j0:j1], gn_sb[:, t : t + 1], gs[t][:, j0:j1], ALU.mult, ALU.subtract
            )

        for t in range(PACK):
            ds.append(keep.tile([P, WIDE], F32, name=f"ds{t}"))
            nc.scalar.activation(ds[t][:].indirect(n2_sb[:]), st[t][:], ACT.Copy)
            if t < PACK - 1:
                make_z(t, 0, S)
        for j0 in (0, HALF):
            make_z(PACK - 1, j0, j0 + HALF)
            nc.vector.quantize_mx(
                out=z_codes[:, j0 : j0 + HALF].bitcast(FP8X4),
                scales=z_plane[:, j0 : j0 + HALF],
                in_=z[:, PACK * j0 : PACK * (j0 + HALF)],
            )

        h = [keep.tile([P, S], F32, name=f"h{m}") for m in range(PACK)]
        ds2 = [keep.tile([P, WIDE], F32, name=f"ds2_{m}") for m in range(PACK)]
        sg = [keep.tile([P, S], F32, name=f"sg{m}") for m in range(PACK)]
        res = [keep.tile([P, S], F32, name=f"res{m}") for m in range(PACK)]

        def product(m, j0, j1):
            acc = psum.tile([P, j1 - j0], F32, name="acc")
            nc.tensor.matmul_mx(
                out=acc[:],
                lhsT=w_codes[:, 2 * P * m : 2 * P * (m + 1)].bitcast(FP4X4),
                lhsT_scale=w_plane[:, P * m : P * (m + 1)],
                rhs=z_codes[:, j0:j1].bitcast(FP8X4),
                rhs_scale=z_plane[:, j0:j1],
                start=True,
                stop=True,
            )
            return acc

        def send(m, j0, j1):
            nc.scalar.activation(ds2[m][:].indirect(n3_sb[:, j0 // 16 : j1 // 16]), h[m][:, j0:j1], ACT.Copy)

        def finish(m, j0, j1):
            nc.scalar.activation(
                sg[m][:, j0:j1],
                ds2[m][:].indirect(n4_sb[:, j0 // 16 : j1 // 16]),
                ACT.Sigmoid,
                bias=bias[:, m : m + 1],
                scale=sl_sb[:, m : m + 1],
            )
            nc.vector.tensor_tensor(res[m][:, j0:j1], h[m][:, j0:j1], sg[m][:, j0:j1], ALU.mult)
            nc.sync.dma_start(out[P * m : P * (m + 1), j0:j1], res[m][:, j0:j1])

        for m in (0, 1):
            nc.scalar.copy(h[m][:, 0:HALF], product(m, 0, HALF)[:])
        for m in (0, 1):
            send(m, 0, HALF)
        for m in (0, 1):
            nc.vector.tensor_copy(h[m][:, HALF:S], product(m, HALF, S)[:])
            send(m, HALF, S)
        finish(0, 0, S)
        for m in range(2, PACK):
            nc.vector.tensor_copy(h[m][:], product(m, 0, S)[:])
            send(m, 0, S)
            finish(m - 1, 0, S)
        finish(PACK - 1, 0, HALF)
        finish(PACK - 1, HALF, S)
